import numpy as np
import ml_dtypes

BF16 = ml_dtypes.bfloat16


def bf(x):
    return np.asarray(x, np.float32).astype(BF16)


def f32(x):
    return np.asarray(x, np.float32)


def f64(x):
    return np.asarray(x).astype(np.float64)


def striped(idx):
    return np.tile(idx.reshape(-1, 16).T, (8, 1))


def rows(idx, k):
    return np.tile(idx, (k, 1))


def look(tab, idx):
    return np.take_along_axis(f64(tab), rows(idx, len(tab)), axis=1)


K, S, V, N, M = 128, 2048, 1024, 1024, 256


def setup_inputs():
    return {"tab": f32(np.random.standard_normal((2, K, S))), "y": f32(np.random.standard_normal((K, V))), "w": bf(np.random.standard_normal((K, M)) / np.sqrt(K)), "b": f32(0.5 * np.random.standard_normal((M, 1))), "offs": striped(np.random.permutation(S)[:N])}


def reference(tab, y, w, b, offs):
    idx = offs[:16].T.reshape(-1)
    x = (look(tab[0], idx) * f64(y)) * (1.0 / (1.0 + np.exp(-look(tab[1], idx))))
    return np.maximum(f64(w).T @ x + f64(b), 0.0)

@@ -1,0 +1,50 @@
+import concourse.mybir as mybir
+
+F32, BF16, U16 = mybir.dt.float32, mybir.dt.bfloat16, mybir.dt.uint16
+MULT = mybir.AluOpType.mult
+SIGMOID, RELU = mybir.ActivationFunctionType.Sigmoid, mybir.ActivationFunctionType.Relu
+
+ROWS, PLACES, ENTRIES, OUTS = 128, 2048, 1024, 256
+HALVES = OUTS // ROWS
+PER_COLUMN = 16
+PIECE = 256
+FLOPS = 2 * ROWS * OUTS * ENTRIES
+
+
+def tile_lookup_vg_mulsig_relu_kernel(tc, tab, y, w, b, offs, out):
+    nc = tc.nc
+    out_rows = out.rearrange("(p h) n -> p h n", h=HALVES)
+    with (
+        tc.tile_pool(name="held", bufs=1) as held,
+        tc.psum_pool(name="psum", bufs=1) as psum,
+    ):
+        offsets = held.tile([ROWS, ENTRIES // PER_COLUMN], U16)
+        gates = held.tile([ROWS, PLACES], F32)
+        values = held.tile([ROWS, PLACES], F32)
+        weights = held.tile([ROWS, OUTS], BF16)
+        bias = held.tile([ROWS, HALVES], F32)
+        starts = range(0, ENTRIES, PIECE)
+        stream = [held.tile([ROWS, PIECE], F32, name=f"stream{s}") for s in starts]
+
+        nc.sync.dma_start(offsets[:], offs)
+        nc.sync.dma_start(gates[:], tab[1])
+        nc.sync.dma_start(values[:], tab[0])
+        for k, s in enumerate(starts):
+            nc.sync.dma_start(stream[k][:], y[:, s : s + PIECE])
+        nc.scalar.dma_start(weights[:], w)
+        nc.scalar.dma_start(bias[:], b.rearrange("(p h) o -> p (h o)", h=HALVES))
+
+        for k, s in enumerate(starts):
+            entries = offsets[:, s // PER_COLUMN : (s + PIECE) // PER_COLUMN]
+            gate = held.tile([ROWS, PIECE], F32, name=f"gate{s}")
+            nc.scalar.activation(gate[:], gates[:].indirect(entries), SIGMOID)
+            product = held.tile([ROWS, PIECE], F32, name=f"product{s}")
+            nc.vector.tensor_tensor(product[:], values[:].indirect(entries), stream[k][:], MULT)
+            x = held.tile([ROWS, PIECE], BF16, name=f"x{s}")
+            nc.vector.tensor_tensor(x[:], product[:], gate[:], MULT)
+            result = held.tile([ROWS, HALVES, PIECE], F32, name=f"result{s}")
+            for h in range(HALVES):
+                sums = psum.tile([ROWS, PIECE], F32, name=f"sums{s}_{h}")
+                nc.tensor.matmul(sums[:], weights[:, h::HALVES], x[:], start=True, stop=True)
+                nc.scalar.activation(result[:, h, :], sums[:], RELU, bias=bias[:, h : h + 1])
+            nc.sync.dma_start(out_rows[:, :, s : s + PIECE], result[:])

@@ -1,50 +1,69 @@
 import concourse.mybir as mybir
 
 F32, BF16, U16 = mybir.dt.float32, mybir.dt.bfloat16, mybir.dt.uint16
-MULT = mybir.AluOpType.mult
+MULT, ADD, MAX = mybir.AluOpType.mult, mybir.AluOpType.add, mybir.AluOpType.max
 SIGMOID, RELU = mybir.ActivationFunctionType.Sigmoid, mybir.ActivationFunctionType.Relu
 
 ROWS, PLACES, ENTRIES, OUTS = 128, 2048, 1024, 256
 HALVES = OUTS // ROWS
 PER_COLUMN = 16
-PIECE = 256
+WIDTHS = [256, 256, 256, 128, 128]
+EARLY = 512
 FLOPS = 2 * ROWS * OUTS * ENTRIES
 
 
 def tile_lookup_vg_mulsig_relu_kernel(tc, tab, y, w, b, offs, out):
     nc = tc.nc
     out_rows = out.rearrange("(p h) n -> p h n", h=HALVES)
+    pieces = [slice(sum(WIDTHS[:k]), sum(WIDTHS[: k + 1])) for k in range(len(WIDTHS))]
+    last = len(pieces) - 1
     with (
         tc.tile_pool(name="held", bufs=1) as held,
-        tc.psum_pool(name="psum", bufs=1) as psum,
+        tc.psum_pool(name="psum", bufs=4) as psum,
     ):
         offsets = held.tile([ROWS, ENTRIES // PER_COLUMN], U16)
         gates = held.tile([ROWS, PLACES], F32)
         values = held.tile([ROWS, PLACES], F32)
+        stream = held.tile([ROWS, ENTRIES], F32)
         weights = held.tile([ROWS, OUTS], BF16)
         bias = held.tile([ROWS, HALVES], F32)
-        starts = range(0, ENTRIES, PIECE)
-        stream = [held.tile([ROWS, PIECE], F32, name=f"stream{s}") for s in starts]
 
-        nc.sync.dma_start(offsets[:], offs)
         nc.sync.dma_start(gates[:], tab[1])
+        nc.sync.dma_start(offsets[:], offs)
+        nc.sync.dma_start(stream[:, :EARLY], y[:, :EARLY])
         nc.sync.dma_start(values[:], tab[0])
-        for k, s in enumerate(starts):
-            nc.sync.dma_start(stream[k][:], y[:, s : s + PIECE])
-        nc.scalar.dma_start(weights[:], w)
-        nc.scalar.dma_start(bias[:], b.rearrange("(p h) o -> p (h o)", h=HALVES))
+        nc.sync.dma_start(stream[:, EARLY:], y[:, EARLY:])
+        nc.sync.dma_start(weights[:], w)
+        nc.sync.dma_start(bias[:], b.rearrange("(p h) o -> p (h o)", h=HALVES))
 
-        for k, s in enumerate(starts):
-            entries = offsets[:, s // PER_COLUMN : (s + PIECE) // PER_COLUMN]
-            gate = held.tile([ROWS, PIECE], F32, name=f"gate{s}")
-            nc.scalar.activation(gate[:], gates[:].indirect(entries), SIGMOID)
-            product = held.tile([ROWS, PIECE], F32, name=f"product{s}")
-            nc.vector.tensor_tensor(product[:], values[:].indirect(entries), stream[k][:], MULT)
-            x = held.tile([ROWS, PIECE], BF16, name=f"x{s}")
-            nc.vector.tensor_tensor(x[:], product[:], gate[:], MULT)
-            result = held.tile([ROWS, HALVES, PIECE], F32, name=f"result{s}")
+        zero = held.tile([ROWS, 1], F32)
+        early_sigmoid = held.tile([ROWS, 1], F32)
+        nc.vector.memset(zero[:], 0.0)
+        nc.scalar.activation(early_sigmoid[:], zero[:], SIGMOID)
+
+        def entries(k):
+            return offsets[:, pieces[k].start // PER_COLUMN : pieces[k].stop // PER_COLUMN]
+
+        gate = held.tile([ROWS, ENTRIES], F32)
+        product = held.tile([ROWS, ENTRIES], F32)
+        x = held.tile([ROWS, ENTRIES], BF16)
+        for k, piece in enumerate(pieces):
+            nc.scalar.activation(gate[:, piece], gates[:].indirect(entries(k)), SIGMOID)
+
+        def look_up_values(k):
+            nc.vector.tensor_tensor(product[:, pieces[k]], values[:].indirect(entries(k)), stream[:, pieces[k]], MULT)
+
+        look_up_values(0)
+        for k, piece in enumerate(pieces):
+            if k < last:
+                look_up_values(k + 1)
+            nc.vector.tensor_tensor(x[:, piece], product[:, piece], gate[:, piece], MULT)
+            result = held.tile([ROWS, HALVES, WIDTHS[k]], F32, name=f"result{k}")
             for h in range(HALVES):
-                sums = psum.tile([ROWS, PIECE], F32, name=f"sums{s}_{h}")
-                nc.tensor.matmul(sums[:], weights[:, h::HALVES], x[:], start=True, stop=True)
-                nc.scalar.activation(result[:, h, :], sums[:], RELU, bias=bias[:, h : h + 1])
-            nc.sync.dma_start(out_rows[:, :, s : s + PIECE], result[:])
+                sums = psum.tile([ROWS, WIDTHS[k]], F32, name=f"sums{h}")
+                nc.tensor.matmul(sums[:], weights[:, h::HALVES], x[:, piece], start=True, stop=True)
+                if k == last and h == HALVES - 1:
+                    nc.vector.tensor_scalar(result[:, h, :], sums[:], bias[:, h : h + 1], 0.0, ADD, MAX)
+                else:
+                    nc.scalar.activation(result[:, h, :], sums[:], RELU, bias=bias[:, h : h + 1])
+            nc.sync.dma_start(out_rows[:, :, piece], result[:])

@@ -7,8 +7,8 @@ SIGMOID, RELU = mybir.ActivationFunctionType.Sigmoid, mybir.ActivationFunctionTy
 ROWS, PLACES, ENTRIES, OUTS = 128, 2048, 1024, 256
 HALVES = OUTS // ROWS
 PER_COLUMN = 16
-WIDTHS = [256, 256, 256, 128, 128]
-EARLY = 512
+WIDTHS = [128] * 8
+EARLY = 256
 FLOPS = 2 * ROWS * OUTS * ENTRIES
 
 
@@ -47,23 +47,35 @@ def tile_lookup_vg_mulsig_relu_kernel(tc, tab, y, w, b, offs, out):
         gate = held.tile([ROWS, ENTRIES], F32)
         product = held.tile([ROWS, ENTRIES], F32)
         x = held.tile([ROWS, ENTRIES], BF16)
+        unread = psum.tile([ROWS, max(WIDTHS)], F32, tag="sums0")
         for k, piece in enumerate(pieces):
             nc.scalar.activation(gate[:, piece], gates[:].indirect(entries(k)), SIGMOID)
+            nc.tensor.matmul(unread[:, : WIDTHS[k]], gate[:, :ROWS], gate[:, piece], start=True, stop=True)
 
         def look_up_values(k):
             nc.vector.tensor_tensor(product[:, pieces[k]], values[:].indirect(entries(k)), stream[:, pieces[k]], MULT)
 
+        def finish(k, sums, shared):
+            result = held.tile([ROWS, HALVES, WIDTHS[k]], F32, name=f"result{k}")
+            nc.scalar.activation(result[:, 0, :], sums[0][:], RELU, bias=bias[:, 0:1])
+            if shared:
+                nc.vector.tensor_scalar(result[:, 1, :], sums[1][:], bias[:, 1:2], 0.0, ADD, MAX)
+            else:
+                nc.scalar.activation(result[:, 1, :], sums[1][:], RELU, bias=bias[:, 1:2])
+            nc.sync.dma_start(out_rows[:, :, pieces[k]], result[:])
+
+        waiting = []
         look_up_values(0)
         for k, piece in enumerate(pieces):
             if k < last:
                 look_up_values(k + 1)
             nc.vector.tensor_tensor(x[:, piece], product[:, piece], gate[:, piece], MULT)
-            result = held.tile([ROWS, HALVES, WIDTHS[k]], F32, name=f"result{k}")
+            sums = [psum.tile([ROWS, WIDTHS[k]], F32, name=f"sums{h}") for h in range(HALVES)]
             for h in range(HALVES):
-                sums = psum.tile([ROWS, WIDTHS[k]], F32, name=f"sums{h}")
-                nc.tensor.matmul(sums[:], weights[:, h::HALVES], x[:, piece], start=True, stop=True)
-                if k == last and h == HALVES - 1:
-                    nc.vector.tensor_scalar(result[:, h, :], sums[:], bias[:, h : h + 1], 0.0, ADD, MAX)
-                else:
-                    nc.scalar.activation(result[:, h, :], sums[:], RELU, bias=bias[:, h : h + 1])
-            nc.sync.dma_start(out_rows[:, :, piece], result[:])
+                nc.tensor.matmul(sums[h][:], weights[:, h::HALVES], x[:, piece], start=True, stop=True)
+            if k < last:
+                finish(k, sums, shared=False)
+            else:
+                waiting.append((k, sums))
+        for k, sums in waiting:
+            finish(k, sums, shared=True)

@@ -7,19 +7,20 @@ SIGMOID, RELU = mybir.ActivationFunctionType.Sigmoid, mybir.ActivationFunctionTy
 ROWS, PLACES, ENTRIES, OUTS = 128, 2048, 1024, 256
 HALVES = OUTS // ROWS
 PER_COLUMN = 16
-WIDTHS = [128] * 8
-EARLY = 256
+PIECE = 128
+EARLY = 2 * PIECE
+BANKS = 8
 FLOPS = 2 * ROWS * OUTS * ENTRIES
 
 
 def tile_lookup_vg_mulsig_relu_kernel(tc, tab, y, w, b, offs, out):
     nc = tc.nc
     out_rows = out.rearrange("(p h) n -> p h n", h=HALVES)
-    pieces = [slice(sum(WIDTHS[:k]), sum(WIDTHS[: k + 1])) for k in range(len(WIDTHS))]
+    pieces = [slice(start, start + PIECE) for start in range(0, ENTRIES, PIECE)]
     last = len(pieces) - 1
     with (
         tc.tile_pool(name="held", bufs=1) as held,
-        tc.psum_pool(name="psum", bufs=4) as psum,
+        tc.psum_pool(name="psum", bufs=BANKS // HALVES) as psum,
     ):
         offsets = held.tile([ROWS, ENTRIES // PER_COLUMN], U16)
         gates = held.tile([ROWS, PLACES], F32)
@@ -36,46 +37,30 @@ def tile_lookup_vg_mulsig_relu_kernel(tc, tab, y, w, b, offs, out):
         nc.sync.dma_start(weights[:], w)
         nc.sync.dma_start(bias[:], b.rearrange("(p h) o -> p (h o)", h=HALVES))
 
-        zero = held.tile([ROWS, 1], F32)
-        early_sigmoid = held.tile([ROWS, 1], F32)
-        nc.vector.memset(zero[:], 0.0)
-        nc.scalar.activation(early_sigmoid[:], zero[:], SIGMOID)
-
-        def entries(k):
-            return offsets[:, pieces[k].start // PER_COLUMN : pieces[k].stop // PER_COLUMN]
+        def entries(piece):
+            return offsets[:, piece.start // PER_COLUMN : piece.stop // PER_COLUMN]
 
         gate = held.tile([ROWS, ENTRIES], F32)
         product = held.tile([ROWS, ENTRIES], F32)
         x = held.tile([ROWS, ENTRIES], BF16)
-        unread = psum.tile([ROWS, max(WIDTHS)], F32, tag="sums0")
-        for k, piece in enumerate(pieces):
-            nc.scalar.activation(gate[:, piece], gates[:].indirect(entries(k)), SIGMOID)
-            nc.tensor.matmul(unread[:, : WIDTHS[k]], gate[:, :ROWS], gate[:, piece], start=True, stop=True)
+        for piece in pieces:
+            nc.scalar.activation(gate[:, piece], gates[:].indirect(entries(piece)), SIGMOID)
 
-        def look_up_values(k):
-            nc.vector.tensor_tensor(product[:, pieces[k]], values[:].indirect(entries(k)), stream[:, pieces[k]], MULT)
+        def look_up_values(piece):
+            nc.vector.tensor_tensor(product[:, piece], values[:].indirect(entries(piece)), stream[:, piece], MULT)
 
-        def finish(k, sums, shared):
-            result = held.tile([ROWS, HALVES, WIDTHS[k]], F32, name=f"result{k}")
-            nc.scalar.activation(result[:, 0, :], sums[0][:], RELU, bias=bias[:, 0:1])
-            if shared:
-                nc.vector.tensor_scalar(result[:, 1, :], sums[1][:], bias[:, 1:2], 0.0, ADD, MAX)
-            else:
-                nc.scalar.activation(result[:, 1, :], sums[1][:], RELU, bias=bias[:, 1:2])
-            nc.sync.dma_start(out_rows[:, :, pieces[k]], result[:])
-
-        waiting = []
-        look_up_values(0)
+        look_up_values(pieces[0])
         for k, piece in enumerate(pieces):
             if k < last:
-                look_up_values(k + 1)
+                look_up_values(pieces[k + 1])
             nc.vector.tensor_tensor(x[:, piece], product[:, piece], gate[:, piece], MULT)
-            sums = [psum.tile([ROWS, WIDTHS[k]], F32, name=f"sums{h}") for h in range(HALVES)]
+            sums = [psum.tile([ROWS, PIECE], F32, name=f"sums{h}") for h in range(HALVES)]
             for h in range(HALVES):
                 nc.tensor.matmul(sums[h][:], weights[:, h::HALVES], x[:, piece], start=True, stop=True)
+            result = held.tile([ROWS, HALVES, PIECE], F32, name=f"result{k}")
+            nc.scalar.activation(result[:, 0, :], sums[0][:], RELU, bias=bias[:, 0:1])
             if k < last:
-                finish(k, sums, shared=False)
+                nc.scalar.activation(result[:, 1, :], sums[1][:], RELU, bias=bias[:, 1:2])
             else:
-                waiting.append((k, sums))
-        for k, sums in waiting:
-            finish(k, sums, shared=True)
+                nc.vector.tensor_scalar(result[:, 1, :], sums[1][:], bias[:, 1:2], 0.0, ADD, MAX)
+            nc.sync.dma_start(out_rows[:, :, piece], result[:])

import concourse.mybir as mybir

F32, BF16, U16 = mybir.dt.float32, mybir.dt.bfloat16, mybir.dt.uint16
MULT, ADD, MAX = mybir.AluOpType.mult, mybir.AluOpType.add, mybir.AluOpType.max
SIGMOID, RELU = mybir.ActivationFunctionType.Sigmoid, mybir.ActivationFunctionType.Relu

ROWS, PLACES, ENTRIES, OUTS = 128, 2048, 1024, 256
HALVES = OUTS // ROWS
PER_COLUMN = 16
PIECE = 128
EARLY = 2 * PIECE
BANKS = 8
FLOPS = 2 * ROWS * OUTS * ENTRIES


def tile_lookup_vg_mulsig_relu_kernel(tc, tab, y, w, b, offs, out):
    nc = tc.nc
    out_rows = out.rearrange("(p h) n -> p h n", h=HALVES)
    pieces = [slice(start, start + PIECE) for start in range(0, ENTRIES, PIECE)]
    last = len(pieces) - 1
    with (
        tc.tile_pool(name="held", bufs=1) as held,
        tc.psum_pool(name="psum", bufs=BANKS // HALVES) as psum,
    ):
        offsets = held.tile([ROWS, ENTRIES // PER_COLUMN], U16)
        gates = held.tile([ROWS, PLACES], F32)
        values = held.tile([ROWS, PLACES], F32)
        stream = held.tile([ROWS, ENTRIES], F32)
        weights = held.tile([ROWS, OUTS], BF16)
        bias = held.tile([ROWS, HALVES], F32)

        nc.sync.dma_start(gates[:], tab[1])
        nc.sync.dma_start(offsets[:], offs)
        nc.sync.dma_start(stream[:, :EARLY], y[:, :EARLY])
        nc.sync.dma_start(values[:], tab[0])
        nc.sync.dma_start(stream[:, EARLY:], y[:, EARLY:])
        nc.sync.dma_start(weights[:], w)
        nc.sync.dma_start(bias[:], b.rearrange("(p h) o -> p (h o)", h=HALVES))

        def entries(piece):
            return offsets[:, piece.start // PER_COLUMN : piece.stop // PER_COLUMN]

        gate = held.tile([ROWS, ENTRIES], F32)
        product = held.tile([ROWS, ENTRIES], F32)
        x = held.tile([ROWS, ENTRIES], BF16)
        for piece in pieces:
            nc.scalar.activation(gate[:, piece], gates[:].indirect(entries(piece)), SIGMOID)

        def look_up_values(piece):
            nc.vector.tensor_tensor(product[:, piece], values[:].indirect(entries(piece)), stream[:, piece], MULT)

        look_up_values(pieces[0])
        for k, piece in enumerate(pieces):
            if k < last:
                look_up_values(pieces[k + 1])
            nc.vector.tensor_tensor(x[:, piece], product[:, piece], gate[:, piece], MULT)
            sums = [psum.tile([ROWS, PIECE], F32, name=f"sums{h}") for h in range(HALVES)]
            for h in range(HALVES):
                nc.tensor.matmul(sums[h][:], weights[:, h::HALVES], x[:, piece], start=True, stop=True)
            result = held.tile([ROWS, HALVES, PIECE], F32, name=f"result{k}")
            nc.scalar.activation(result[:, 0, :], sums[0][:], RELU, bias=bias[:, 0:1])
            if k < last:
                nc.scalar.activation(result[:, 1, :], sums[1][:], RELU, bias=bias[:, 1:2])
            else:
                nc.vector.tensor_scalar(result[:, 1, :], sums[1][:], bias[:, 1:2], 0.0, ADD, MAX)
            nc.sync.dma_start(out_rows[:, :, piece], result[:])
